import numpy as np
import ml_dtypes


def mxq(x, axis, fmt="e4m3"):
    dtype, down = {"e4m3": (ml_dtypes.float8_e4m3fn, 7), "e5m2": (ml_dtypes.float8_e5m2, 14)}[fmt]
    v = np.moveaxis(np.asarray(x, np.float32).astype(ml_dtypes.bfloat16).astype(np.float64), axis, -1)
    blocks = v.reshape(v.shape[:-1] + (-1, 32))
    amax = np.abs(blocks).max(-1, keepdims=True)
    byte = np.maximum(np.where(amax > 0, np.frexp(amax)[1] - 1 + 127, 0) - down, 1)
    scale = np.exp2(byte - 127.0)
    codes = (blocks / scale).astype(np.float32).astype(dtype).astype(np.float64)
    return np.moveaxis((codes * scale).reshape(v.shape), -1, axis)


WIDE = False


def mx_kscale(k):
    if not WIDE:
        return np.ones(k)
    levels = np.array([24, -24, 12, -12, 0])
    if k % 512:
        return np.exp2(np.random.permutation(np.resize(levels, k // 32))).repeat(32)
    a = np.empty((k // 512, 16))
    for p in range(k // 512):
        a[p, :8] = np.random.permutation(np.resize(levels, 8))
        for g in range(8):
            far = levels[np.abs(levels - a[p, g]) >= 10]
            a[p, g + 8] = far[np.random.randint(len(far))]
    return np.exp2(a.ravel()).repeat(32)


def f64(x):
    return np.asarray(x).astype(np.float64)


E2M1 = np.array([0.0, 0.5, 1.0, 1.5, 2.0, 3.0, 4.0, 6.0, -0.0, -0.5, -1.0, -1.5, -2.0, -3.0, -4.0, -6.0])


def pack_weight(w, fmt):
    k, n = w.shape
    w = f64(np.asarray(w, np.float32).astype(ml_dtypes.bfloat16)).reshape(k // 32, 32, n)
    amax = np.abs(w).max(1)
    if fmt == "e4m3":
        byte = np.frexp(amax)[1] - 1 + 127 - 7
    else:
        mant, ex = np.frexp(amax / 6.0)
        byte = np.where(mant > 0.5, ex, ex - 1) + 127
    byte = np.clip(np.where(amax > 0, byte, 1), 1, 254)
    scaled = (w * np.exp2(127.0 - byte)[:, None, :]).reshape(k, n).astype(np.float32)
    by_word = np.ascontiguousarray(scaled.reshape(k // 512, 128, 4, n).transpose(0, 1, 3, 2))
    if fmt == "e4m3":
        words = by_word.astype(ml_dtypes.float8_e4m3fn).view(np.uint8)
    else:
        c = by_word.astype(ml_dtypes.float4_e2m1fn).view(np.uint8) & 0xF
        words = (c[..., 0::2] | (c[..., 1::2] << 4)).reshape(k // 512, 128, 2 * n)
    return np.ascontiguousarray(words), np.ascontiguousarray(byte.astype(np.uint8).reshape(k // 512, 16, n))


def unpack_weight(words, scales, fmt):
    g, _, n = scales.shape
    words = np.ascontiguousarray(words).reshape(g, 128, n, -1)
    if fmt == "e4m3":
        vals = words.view(ml_dtypes.float8_e4m3fn).astype(np.float64)
    else:
        nib = np.empty((g, 128, n, 4), np.uint8)
        nib[..., 0::2] = words & 0xF
        nib[..., 1::2] = words >> 4
        vals = E2M1[nib]
    vals = vals * np.repeat(np.exp2(scales.astype(np.float64) - 127.0), 8, axis=1)[..., None]
    return vals.transpose(0, 1, 3, 2).reshape(g * 512, n)


def planes(y):
    n, m = y.shape
    v = y.astype(np.float32).astype(ml_dtypes.bfloat16).astype(np.float64).reshape(n // 32, 32, m)
    top = np.abs(v).max(1)
    byte = np.clip(np.where(top > 0, np.frexp(top)[1] - 1 + 127 - 7, 1), 1, 254)
    codes = (v * np.exp2(127.0 - byte)[:, None, :]).reshape(n, m).astype(np.float32).astype(ml_dtypes.float8_e4m3fn).view(np.uint8)
    words = codes.reshape(n // 512, 128, 4, m).transpose(0, 1, 3, 2)
    return np.ascontiguousarray(words), np.ascontiguousarray(byte.astype(np.uint8).reshape(n // 512, 16, m))


K, L, R, N, T = 512, 1024, 512, 512, 1536


def setup_inputs():
    n = np.random.standard_normal
    u = mx_kscale(R)[:, None]
    s = mx_kscale(K)[:, None]
    s2 = mx_kscale(L)[:, None]
    p_w4 = pack_weight(n((K, R)) / np.sqrt(K) / s * u.T, "e2m1")
    p_w8 = pack_weight(n((L, R)) / np.sqrt(L) / s2 * u.T, "e4m3")
    p_v8 = pack_weight(n((R, N)) / np.sqrt(R) / u, "e4m3")
    return {
        "x": (n((K, T)) * s).astype(np.float32),
        "c": (n((L, T)) * s2).astype(np.float32),
        "w4_words": p_w4[0],
        "w4_scales": p_w4[1],
        "w8_words": p_w8[0],
        "w8_scales": p_w8[1],
        "v8_words": p_v8[0],
        "v8_scales": p_v8[1],
        "res": (n((N, T))).astype(np.float32),
    }


def reference(x, c, w4_words, w4_scales, w8_words, w8_scales, v8_words, v8_scales, res):
    x_ = mxq(f64(x), 0, "e4m3")
    c_ = mxq(f64(c), 0, "e4m3")
    w4_ = unpack_weight(w4_words, w4_scales, "e2m1")
    w8_ = unpack_weight(w8_words, w8_scales, "e4m3")
    a = w4_.T @ x_ + w8_.T @ c_
    h = np.maximum(a, 0.0)
    h_ = mxq(h, 0, "e4m3")
    v8_ = unpack_weight(v8_words, v8_scales, "e4m3")
    y = v8_.T @ h_
    return (f64(res) + y, h) + planes(h)

@@ -1,0 +1,230 @@
+from contextlib import ExitStack
+
+import concourse.mybir as mybir
+
+K, L, R, N, T = 512, 1024, 512, 512, 1536
+FLOPS = 2 * T * (K * R + L * R + R * N)
+
+F32 = mybir.dt.float32
+BF16 = mybir.dt.bfloat16
+I32 = mybir.dt.int32
+U32 = mybir.dt.uint32
+U8 = mybir.dt.uint8
+FP8X4 = mybir.dt.float8_e4m3fn_x4
+FP4X4 = mybir.dt.float4_e2m1fn_x4
+
+P = 128
+PACK = 4
+K_PASS = P * PACK
+CHUNK = 512
+CHUNKS = T // CHUNK
+QUADS = 4
+STREAMS = 3
+
+
+def tile_mix_saveskip_relu_res_kernel(
+    tc, x, c, w4_words, w4_scales, w8_words, w8_scales, v8_words, v8_scales, res, out_0, out_1, out_2, out_3
+):
+    nc = tc.nc
+    with ExitStack() as ctx:
+        keep = ctx.enter_context(tc.tile_pool(name="keep", bufs=1))
+        stage = ctx.enter_context(tc.tile_pool(name="stage", bufs=6))
+        psum_a = ctx.enter_context(tc.psum_pool(name="psum_a", bufs=1))
+        psum_y = ctx.enter_context(tc.psum_pool(name="psum_y", bufs=4))
+        ctx.enter_context(tc.manual_schedule())
+
+        def cols(i):
+            return slice(i * CHUNK, (i + 1) * CHUNK)
+
+        w8_raw = keep.tile([P, 2, R], U32, name="w8_raw", align_bytes=64)
+        w8_raw_sc = keep.tile([P, 2, R], U8, name="w8_raw_sc", align_bytes=64)
+        w4_raw = keep.tile([P, 2 * R], U8, name="w4_raw", align_bytes=64)
+        w4_raw_sc = keep.tile([P, 1, R], U8, name="w4_raw_sc", align_bytes=64)
+        w8 = keep.tile([P, 2, R], U32, name="w8", align_bytes=64)
+        w8_sc = keep.tile([P, 2, R], U8, name="w8_sc", align_bytes=64)
+        w4 = keep.tile([P, 2 * R], U8, name="w4", align_bytes=64)
+        w4_sc = keep.tile([P, 1, R], U8, name="w4_sc", align_bytes=64)
+        v8 = keep.tile([P, N], U32, name="v8", align_bytes=64)
+        v8_sc = keep.tile([P, 1, N], U8, name="v8_sc", align_bytes=64)
+
+        raw = {}
+        codes = {}
+        scales = {}
+        for i in range(CHUNKS):
+            for s in range(STREAMS):
+                raw[i, s] = keep.tile([P, PACK, CHUNK], F32, name="raw_%d_%d" % (i, s), align_bytes=64)
+                codes[i, s] = keep.tile([P, CHUNK], U32, name="codes_%d_%d" % (i, s), align_bytes=64)
+                scales[i, s] = keep.tile([P, CHUNK], U8, name="scales_%d_%d" % (i, s), align_bytes=64)
+        acc = [keep.tile([P, T], F32, name="acc_%d" % j, align_bytes=64) for j in range(PACK)]
+        h_early = keep.tile([P, PACK, T - CHUNK], F32, name="h_early", align_bytes=64)
+        h_last = keep.tile([P, PACK, CHUNK], F32, name="h_last", align_bytes=64)
+        h_codes = keep.tile([P, T], U32, name="h_codes", align_bytes=64)
+        h_sc = keep.tile([P, T], U8, name="h_sc", align_bytes=64)
+
+        def h_chunk(i):
+            return h_last[:] if i == CHUNKS - 1 else h_early[:, :, cols(i)]
+
+        stream_rows = [c[0:K_PASS, :], c[K_PASS:L, :], x]
+
+        def load_stream(i, s):
+            nc.sync.dma_start(out=raw[i, s][:], in_=stream_rows[s][:, cols(i)].rearrange("(p j) t -> p j t", j=PACK))
+
+        def load_scale_rows(plane, dram, q):
+            nc.sync.dma_start(
+                out=plane[32 * q : 32 * q + 4, :, :].bitcast(I32),
+                in_=dram.bitcast(I32)[:, 4 * q : 4 * q + 4, :].rearrange("a r n -> r a n"),
+            )
+
+        for plane in (w8_raw_sc, w4_raw_sc, v8_sc):
+            nc.vector.memset(plane[:].bitcast(I32), 0)
+
+        nc.sync.dma_start(out=w8_raw[:].bitcast(I32), in_=w8_words.rearrange("a p r i -> p a (r i)").bitcast(I32))
+        load_stream(0, 0)
+        load_scale_rows(w8_raw_sc, w8_scales, 0)
+        load_scale_rows(w8_raw_sc, w8_scales, 1)
+        load_stream(0, 1)
+        load_scale_rows(w8_raw_sc, w8_scales, 2)
+        load_scale_rows(w8_raw_sc, w8_scales, 3)
+        load_stream(0, 2)
+        nc.sync.dma_start(out=w4_raw[:].bitcast(I32), in_=w4_words[0].bitcast(I32))
+        load_scale_rows(w4_raw_sc, w4_scales, 0)
+        load_scale_rows(w4_raw_sc, w4_scales, 1)
+        load_stream(1, 0)
+        load_scale_rows(w4_raw_sc, w4_scales, 2)
+        load_scale_rows(w4_raw_sc, w4_scales, 3)
+        load_stream(1, 1)
+        load_stream(1, 2)
+        nc.sync.dma_start(out=v8[:].bitcast(I32), in_=v8_words[0].rearrange("p n i -> p (n i)").bitcast(I32))
+        load_scale_rows(v8_sc, v8_scales, 0)
+        load_scale_rows(v8_sc, v8_scales, 1)
+        load_stream(2, 0)
+        load_scale_rows(v8_sc, v8_scales, 2)
+        load_scale_rows(v8_sc, v8_scales, 3)
+        load_stream(2, 1)
+        load_stream(2, 2)
+        for j in range(PACK):
+            nc.sync.dma_start(out=acc[j][:], in_=res[j * P : (j + 1) * P, :])
+
+        grouped = {}
+
+        def interleave(key, src, on_scalar):
+            grouped[key] = stage.tile([P, CHUNK, PACK], BF16, name="grouped", align_bytes=64)
+            dst_view = grouped[key][:].rearrange("p (g i) j -> p g j i", i=4)
+            src_view = src.rearrange("p j (g i) -> p g j i", i=4)
+            if on_scalar:
+                nc.scalar.copy(out=dst_view, in_=src_view)
+            else:
+                nc.vector.tensor_copy(out=dst_view, in_=src_view)
+
+        def quantize(key, words, plane):
+            nc.vector.quantize_mx(
+                out=words.bitcast(FP8X4), scales=plane, in_=grouped[key][:].rearrange("p t j -> p (t j)")
+            )
+
+        def deal_scales(dst, src):
+            nc.vector.tensor_copy(
+                out=dst[:].rearrange("p a (j g i) -> p a g j i", j=PACK, i=16),
+                in_=src[:].rearrange("p a (g i j) -> p a g j i", j=PACK, i=16),
+            )
+
+        banks = {}
+
+        def first_layer_pass(i, s):
+            for j in range(PACK):
+                tile_cols = slice(j * P, (j + 1) * P)
+                if s == 0:
+                    banks[i, j] = psum_a.tile([P, CHUNK], F32, name="a_%d" % j)
+                if s < 2:
+                    weights = w8[:, s, tile_cols].bitcast(FP8X4)
+                    weight_scales = w8_sc[:, s, tile_cols]
+                else:
+                    weights = w4[:, 2 * j * P : 2 * (j + 1) * P].bitcast(FP4X4)
+                    weight_scales = w4_sc[:, 0, tile_cols]
+                nc.tensor.matmul_mx(
+                    out=banks[i, j][:],
+                    lhsT=weights,
+                    lhsT_scale=weight_scales,
+                    rhs=codes[i, s][:].bitcast(FP8X4),
+                    rhs_scale=scales[i, s][:],
+                    start=(s == 0),
+                    stop=(s == STREAMS - 1),
+                )
+
+        def relu(i):
+            for j in range(PACK):
+                nc.scalar.activation(
+                    out=h_chunk(i)[:, j, :], in_=banks[i, j][:], func=mybir.ActivationFunctionType.Relu
+                )
+
+        def second_layer(j, i):
+            y = psum_y.tile([P, CHUNK], F32, name="y")
+            nc.tensor.matmul_mx(
+                out=y[:],
+                lhsT=v8[:, j * P : (j + 1) * P].bitcast(FP8X4),
+                lhsT_scale=v8_sc[:, 0, j * P : (j + 1) * P],
+                rhs=h_codes[:, cols(i)].bitcast(FP8X4),
+                rhs_scale=h_sc[:, cols(i)],
+                start=True,
+                stop=True,
+            )
+            nc.vector.tensor_tensor(
+                out=acc[j][:, cols(i)], in0=y[:], in1=acc[j][:, cols(i)], op=mybir.AluOpType.add
+            )
+
+        def quantize_stream(i, s):
+            quantize((i, s), codes[i, s][:], scales[i, s][:])
+
+        def quantize_h(i):
+            quantize((i, "h"), h_codes[:, cols(i)], h_sc[:, cols(i)])
+
+        nc.vector.tensor_copy(
+            out=w8[:].bitcast(I32).rearrange("p a (j g i) -> p a g j i", j=PACK, i=4),
+            in_=w8_raw[:].bitcast(I32).rearrange("p a (g i j) -> p a g j i", j=PACK, i=4),
+        )
+        for i in range(CHUNKS):
+            interleave((i, 0), raw[i, 0][:], True)
+            if i > 0:
+                relu(i - 1)
+            interleave((i, 1), raw[i, 1][:], False)
+            quantize_stream(i, 0)
+            if i == 0:
+                deal_scales(w8_sc, w8_raw_sc)
+            quantize_stream(i, 1)
+            first_layer_pass(i, 0)
+            first_layer_pass(i, 1)
+            interleave((i, 2), raw[i, 2][:], False)
+            if i == 0:
+                nc.vector.tensor_copy(
+                    out=w4[:].rearrange("p (j g i b) -> p g j i b", j=PACK, i=8, b=2),
+                    in_=w4_raw[:].rearrange("p (g i j b) -> p g j i b", j=PACK, i=8, b=2),
+                )
+            else:
+                interleave((i - 1, "h"), h_chunk(i - 1), False)
+            quantize_stream(i, 2)
+            if i == 0:
+                deal_scales(w4_sc, w4_raw_sc)
+            else:
+                quantize_h(i - 1)
+            first_layer_pass(i, 2)
+
+        last = CHUNKS - 1
+        relu(last)
+        for j in range(PACK - 1):
+            for i in range(last):
+                second_layer(j, i)
+        interleave((last, "h"), h_chunk(last), False)
+        second_layer(PACK - 1, 0)
+        quantize_h(last)
+        second_layer(PACK - 1, 1)
+        for j in range(PACK):
+            second_layer(j, last)
+
+        h_rows = out_1.rearrange("(p j) t -> p j t", j=PACK)
+        nc.sync.dma_start(out=h_rows[:, :, 0 : T - CHUNK], in_=h_early[:])
+        nc.sync.dma_start(out=h_rows[:, :, cols(last)], in_=h_last[:])
+        nc.sync.dma_start(out=out_2[0].rearrange("p t i -> p (t i)").bitcast(I32), in_=h_codes[:].bitcast(I32))
+        for j in range(PACK):
+            nc.sync.dma_start(
+                out=out_3[0].bitcast(I32)[4 * j : 4 * j + 4, :], in_=h_sc[32 * j : 32 * j + 4, :].bitcast(I32)
+            )
+            nc.sync.dma_start(out=out_0[j * P : (j + 1) * P, :], in_=acc[j][:])

@@ -29,8 +29,7 @@ def tile_mix_saveskip_relu_res_kernel(
     with ExitStack() as ctx:
         keep = ctx.enter_context(tc.tile_pool(name="keep", bufs=1))
         stage = ctx.enter_context(tc.tile_pool(name="stage", bufs=6))
-        psum_a = ctx.enter_context(tc.psum_pool(name="psum_a", bufs=1))
-        psum_y = ctx.enter_context(tc.psum_pool(name="psum_y", bufs=4))
+        psum = ctx.enter_context(tc.psum_pool(name="psum", bufs=1))
         ctx.enter_context(tc.manual_schedule())
 
         def cols(i):
@@ -47,27 +46,34 @@ def tile_mix_saveskip_relu_res_kernel(
         v8 = keep.tile([P, N], U32, name="v8", align_bytes=64)
         v8_sc = keep.tile([P, 1, N], U8, name="v8_sc", align_bytes=64)
 
-        raw = {}
+        raw = [keep.tile([P, PACK, T], F32, name="raw_%d" % s, align_bytes=64) for s in range(STREAMS - 1)]
+        x_first = keep.tile([P, PACK, CHUNK], F32, name="x_first", align_bytes=64)
+        x_rest = keep.tile([P, PACK, T - CHUNK], F32, name="x_rest", align_bytes=64)
         codes = {}
         scales = {}
         for i in range(CHUNKS):
             for s in range(STREAMS):
-                raw[i, s] = keep.tile([P, PACK, CHUNK], F32, name="raw_%d_%d" % (i, s), align_bytes=64)
                 codes[i, s] = keep.tile([P, CHUNK], U32, name="codes_%d_%d" % (i, s), align_bytes=64)
                 scales[i, s] = keep.tile([P, CHUNK], U8, name="scales_%d_%d" % (i, s), align_bytes=64)
-        acc = [keep.tile([P, T], F32, name="acc_%d" % j, align_bytes=64) for j in range(PACK)]
-        h_early = keep.tile([P, PACK, T - CHUNK], F32, name="h_early", align_bytes=64)
-        h_last = keep.tile([P, PACK, CHUNK], F32, name="h_last", align_bytes=64)
+        acc = keep.tile([P, PACK, T], F32, name="acc", align_bytes=64)
+        h_first = keep.tile([P, PACK, CHUNK], F32, name="h_first", align_bytes=64)
+        h_rest = keep.tile([P, PACK, T - CHUNK], F32, name="h_rest", align_bytes=64)
         h_codes = keep.tile([P, T], U32, name="h_codes", align_bytes=64)
         h_sc = keep.tile([P, T], U8, name="h_sc", align_bytes=64)
 
         def h_chunk(i):
-            return h_last[:] if i == CHUNKS - 1 else h_early[:, :, cols(i)]
+            return h_first[:] if i == 0 else h_rest[:, :, cols(i - 1)]
 
-        stream_rows = [c[0:K_PASS, :], c[K_PASS:L, :], x]
+        def raw_chunk(i, s):
+            if s < 2:
+                return raw[s][:, :, cols(i)]
+            return x_first[:] if i == 0 else x_rest[:, :, cols(i - 1)]
 
-        def load_stream(i, s):
-            nc.sync.dma_start(out=raw[i, s][:], in_=stream_rows[s][:, cols(i)].rearrange("(p j) t -> p j t", j=PACK))
+        stream_rows = [c[0:K_PASS, :], c[K_PASS:L, :]]
+        x_rows = x.rearrange("(p j) t -> p j t", j=PACK)
+
+        def load_stream(s):
+            nc.sync.dma_start(out=raw[s][:], in_=stream_rows[s].rearrange("(p j) t -> p j t", j=PACK))
 
         def load_scale_rows(plane, dram, q):
             nc.sync.dma_start(
@@ -79,31 +85,19 @@ def tile_mix_saveskip_relu_res_kernel(
             nc.vector.memset(plane[:].bitcast(I32), 0)
 
         nc.sync.dma_start(out=w8_raw[:].bitcast(I32), in_=w8_words.rearrange("a p r i -> p a (r i)").bitcast(I32))
-        load_stream(0, 0)
-        load_scale_rows(w8_raw_sc, w8_scales, 0)
-        load_scale_rows(w8_raw_sc, w8_scales, 1)
-        load_stream(0, 1)
-        load_scale_rows(w8_raw_sc, w8_scales, 2)
-        load_scale_rows(w8_raw_sc, w8_scales, 3)
-        load_stream(0, 2)
+        load_stream(0)
+        for q in range(QUADS):
+            load_scale_rows(w8_raw_sc, w8_scales, q)
         nc.sync.dma_start(out=w4_raw[:].bitcast(I32), in_=w4_words[0].bitcast(I32))
-        load_scale_rows(w4_raw_sc, w4_scales, 0)
-        load_scale_rows(w4_raw_sc, w4_scales, 1)
-        load_stream(1, 0)
-        load_scale_rows(w4_raw_sc, w4_scales, 2)
-        load_scale_rows(w4_raw_sc, w4_scales, 3)
-        load_stream(1, 1)
-        load_stream(1, 2)
+        load_stream(1)
+        for q in range(QUADS):
+            load_scale_rows(w4_raw_sc, w4_scales, q)
+        nc.sync.dma_start(out=x_first[:], in_=x_rows[:, :, 0:CHUNK])
+        nc.sync.dma_start(out=x_rest[:], in_=x_rows[:, :, CHUNK:T])
         nc.sync.dma_start(out=v8[:].bitcast(I32), in_=v8_words[0].rearrange("p n i -> p (n i)").bitcast(I32))
-        load_scale_rows(v8_sc, v8_scales, 0)
-        load_scale_rows(v8_sc, v8_scales, 1)
-        load_stream(2, 0)
-        load_scale_rows(v8_sc, v8_scales, 2)
-        load_scale_rows(v8_sc, v8_scales, 3)
-        load_stream(2, 1)
-        load_stream(2, 2)
-        for j in range(PACK):
-            nc.sync.dma_start(out=acc[j][:], in_=res[j * P : (j + 1) * P, :])
+        for q in range(QUADS):
+            load_scale_rows(v8_sc, v8_scales, q)
+        nc.sync.dma_start(out=acc[:], in_=res.rearrange("(j p) t -> p j t", p=P))
 
         grouped = {}
 
@@ -129,35 +123,40 @@ def tile_mix_saveskip_relu_res_kernel(
 
         banks = {}
 
+        def first_layer(i, s, j):
+            tile_cols = slice(j * P, (j + 1) * P)
+            if s == 0:
+                banks[i, j] = psum.tile([P, CHUNK], F32, name="bank_%d_%d" % (i % 2, j))
+            if s < 2:
+                weights = w8[:, s, tile_cols].bitcast(FP8X4)
+                weight_scales = w8_sc[:, s, tile_cols]
+            else:
+                weights = w4[:, 2 * j * P : 2 * (j + 1) * P].bitcast(FP4X4)
+                weight_scales = w4_sc[:, 0, tile_cols]
+            nc.tensor.matmul_mx(
+                out=banks[i, j][:],
+                lhsT=weights,
+                lhsT_scale=weight_scales,
+                rhs=codes[i, s][:].bitcast(FP8X4),
+                rhs_scale=scales[i, s][:],
+                start=(s == 0),
+                stop=(s == STREAMS - 1),
+            )
+
         def first_layer_pass(i, s):
             for j in range(PACK):
-                tile_cols = slice(j * P, (j + 1) * P)
-                if s == 0:
-                    banks[i, j] = psum_a.tile([P, CHUNK], F32, name="a_%d" % j)
-                if s < 2:
-                    weights = w8[:, s, tile_cols].bitcast(FP8X4)
-                    weight_scales = w8_sc[:, s, tile_cols]
-                else:
-                    weights = w4[:, 2 * j * P : 2 * (j + 1) * P].bitcast(FP4X4)
-                    weight_scales = w4_sc[:, 0, tile_cols]
-                nc.tensor.matmul_mx(
-                    out=banks[i, j][:],
-                    lhsT=weights,
-                    lhsT_scale=weight_scales,
-                    rhs=codes[i, s][:].bitcast(FP8X4),
-                    rhs_scale=scales[i, s][:],
-                    start=(s == 0),
-                    stop=(s == STREAMS - 1),
-                )
+                first_layer(i, s, j)
 
-        def relu(i):
-            for j in range(PACK):
+        def relu(i, j, on_scalar):
+            if on_scalar:
                 nc.scalar.activation(
                     out=h_chunk(i)[:, j, :], in_=banks[i, j][:], func=mybir.ActivationFunctionType.Relu
                 )
+            else:
+                nc.vector.tensor_scalar_max(out=h_chunk(i)[:, j, :], in0=banks[i, j][:], scalar1=0.0)
 
-        def second_layer(j, i):
-            y = psum_y.tile([P, CHUNK], F32, name="y")
+        def second_layer(j, i, bank):
+            y = psum.tile([P, CHUNK], F32, name="bank_1_%d" % bank)
             nc.tensor.matmul_mx(
                 out=y[:],
                 lhsT=v8[:, j * P : (j + 1) * P].bitcast(FP8X4),
@@ -168,8 +167,11 @@ def tile_mix_saveskip_relu_res_kernel(
                 stop=True,
             )
             nc.vector.tensor_tensor(
-                out=acc[j][:, cols(i)], in0=y[:], in1=acc[j][:, cols(i)], op=mybir.AluOpType.add
+                out=acc[:, j, cols(i)], in0=y[:], in1=acc[:, j, cols(i)], op=mybir.AluOpType.add
             )
+
+        def interleave_stream(i, s, on_scalar):
+            interleave((i, s), raw_chunk(i, s), on_scalar)
 
         def quantize_stream(i, s):
             quantize((i, s), codes[i, s][:], scales[i, s][:])
@@ -181,50 +183,65 @@ def tile_mix_saveskip_relu_res_kernel(
             out=w8[:].bitcast(I32).rearrange("p a (j g i) -> p a g j i", j=PACK, i=4),
             in_=w8_raw[:].bitcast(I32).rearrange("p a (g i j) -> p a g j i", j=PACK, i=4),
         )
-        for i in range(CHUNKS):
-            interleave((i, 0), raw[i, 0][:], True)
-            if i > 0:
-                relu(i - 1)
-            interleave((i, 1), raw[i, 1][:], False)
-            quantize_stream(i, 0)
-            if i == 0:
-                deal_scales(w8_sc, w8_raw_sc)
-            quantize_stream(i, 1)
-            first_layer_pass(i, 0)
-            first_layer_pass(i, 1)
-            interleave((i, 2), raw[i, 2][:], False)
-            if i == 0:
-                nc.vector.tensor_copy(
-                    out=w4[:].rearrange("p (j g i b) -> p g j i b", j=PACK, i=8, b=2),
-                    in_=w4_raw[:].rearrange("p (g i j b) -> p g j i b", j=PACK, i=8, b=2),
-                )
-            else:
-                interleave((i - 1, "h"), h_chunk(i - 1), False)
-            quantize_stream(i, 2)
-            if i == 0:
-                deal_scales(w4_sc, w4_raw_sc)
-            else:
-                quantize_h(i - 1)
-            first_layer_pass(i, 2)
+        interleave_stream(1, 0, True)
+        interleave_stream(2, 0, True)
+        interleave_stream(0, 0, False)
+        deal_scales(w8_sc, w8_raw_sc)
+        quantize_stream(0, 0)
+        nc.vector.tensor_copy(
+            out=w4[:].rearrange("p (j g i b) -> p g j i b", j=PACK, i=8, b=2),
+            in_=w4_raw[:].rearrange("p (g i j b) -> p g j i b", j=PACK, i=8, b=2),
+        )
+        quantize_stream(1, 0)
+        quantize_stream(2, 0)
+        first_layer_pass(0, 0)
+        first_layer_pass(1, 0)
 
-        last = CHUNKS - 1
-        relu(last)
-        for j in range(PACK - 1):
-            for i in range(last):
-                second_layer(j, i)
-        interleave((last, "h"), h_chunk(last), False)
-        second_layer(PACK - 1, 0)
-        quantize_h(last)
-        second_layer(PACK - 1, 1)
+        interleave_stream(1, 1, True)
+        interleave_stream(2, 1, True)
+        interleave_stream(0, 1, False)
+        deal_scales(w4_sc, w4_raw_sc)
+        quantize_stream(0, 1)
+        first_layer_pass(0, 1)
+        interleave_stream(0, 2, False)
+        quantize_stream(1, 1)
+        first_layer_pass(1, 1)
+        quantize_stream(0, 2)
+        quantize_stream(2, 1)
+        first_layer_pass(0, 2)
         for j in range(PACK):
-            second_layer(j, last)
+            relu(0, j, True)
+        first_layer_pass(2, 0)
+        first_layer_pass(2, 1)
+        interleave((0, "h"), h_chunk(0), True)
+        for i in (1, 2):
+            interleave_stream(i, 2, False)
+            quantize_stream(i, 2)
+            first_layer_pass(i, 2)
+        quantize_h(0)
+        for j in range(PACK):
+            relu(1, j, True)
+        for j in range(PACK):
+            relu(2, j, j % 2 == 1)
+        interleave((1, "h"), h_chunk(1), False)
+        interleave((2, "h"), h_chunk(2), True)
+        second_layer(0, 0, 0)
+        quantize_h(1)
+        second_layer(1, 0, 1)
+        second_layer(0, 1, 2)
+        quantize_h(2)
+        second_layer(1, 1, 3)
+        second_layer(0, 2, 0)
+        second_layer(1, 2, 1)
+        for n in range(2 * CHUNKS):
+            second_layer(2 + n // CHUNKS, n % CHUNKS, (2 + n) % PACK)
 
         h_rows = out_1.rearrange("(p j) t -> p j t", j=PACK)
-        nc.sync.dma_start(out=h_rows[:, :, 0 : T - CHUNK], in_=h_early[:])
-        nc.sync.dma_start(out=h_rows[:, :, cols(last)], in_=h_last[:])
+        nc.sync.dma_start(out=h_rows[:, :, 0:CHUNK], in_=h_first[:])
+        nc.sync.dma_start(out=h_rows[:, :, CHUNK:T], in_=h_rest[:])
         nc.sync.dma_start(out=out_2[0].rearrange("p t i -> p (t i)").bitcast(I32), in_=h_codes[:].bitcast(I32))
         for j in range(PACK):
             nc.sync.dma_start(
                 out=out_3[0].bitcast(I32)[4 * j : 4 * j + 4, :], in_=h_sc[32 * j : 32 * j + 4, :].bitcast(I32)
             )
-            nc.sync.dma_start(out=out_0[j * P : (j + 1) * P, :], in_=acc[j][:])
+            nc.sync.dma_start(out=out_0[j * P : (j + 1) * P, :], in_=acc[:, j, :])

@@ -18,7 +18,9 @@ PACK = 4
 K_PASS = P * PACK
 CHUNK = 512
 CHUNKS = T // CHUNK
-QUADS = 4
+W8_PLANE = 12
+V8_PLANE = 8
+H_PLANE = 4
 STREAMS = 3
 
 
@@ -75,28 +77,26 @@ def tile_mix_saveskip_relu_res_kernel(
         def load_stream(s):
             nc.sync.dma_start(out=raw[s][:], in_=stream_rows[s].rearrange("(p j) t -> p j t", j=PACK))
 
-        def load_scale_rows(plane, dram, q):
-            nc.sync.dma_start(
-                out=plane[32 * q : 32 * q + 4, :, :].bitcast(I32),
-                in_=dram.bitcast(I32)[:, 4 * q : 4 * q + 4, :].rearrange("a r n -> r a n"),
-            )
+        def load_scale_rows(plane, first, dram):
+            for r in range(4):
+                nc.gpsimd.dma_start(
+                    out=plane[first + r : P : 32, :, :].bitcast(I32),
+                    in_=dram.bitcast(I32)[:, r:16:4, :].rearrange("a q n -> q a n"),
+                )
 
         for plane in (w8_raw_sc, w4_raw_sc, v8_sc):
             nc.vector.memset(plane[:].bitcast(I32), 0)
+        load_scale_rows(w8_raw_sc, W8_PLANE, w8_scales)
+        load_scale_rows(w4_raw_sc, 0, w4_scales)
+        load_scale_rows(v8_sc, V8_PLANE, v8_scales)
 
         nc.sync.dma_start(out=w8_raw[:].bitcast(I32), in_=w8_words.rearrange("a p r i -> p a (r i)").bitcast(I32))
         load_stream(0)
-        for q in range(QUADS):
-            load_scale_rows(w8_raw_sc, w8_scales, q)
         nc.sync.dma_start(out=w4_raw[:].bitcast(I32), in_=w4_words[0].bitcast(I32))
         load_stream(1)
-        for q in range(QUADS):
-            load_scale_rows(w4_raw_sc, w4_scales, q)
         nc.sync.dma_start(out=x_first[:], in_=x_rows[:, :, 0:CHUNK])
         nc.sync.dma_start(out=x_rest[:], in_=x_rows[:, :, CHUNK:T])
         nc.sync.dma_start(out=v8[:].bitcast(I32), in_=v8_words[0].rearrange("p n i -> p (n i)").bitcast(I32))
-        for q in range(QUADS):
-            load_scale_rows(v8_sc, v8_scales, q)
         nc.sync.dma_start(out=acc[:], in_=res.rearrange("(j p) t -> p j t", p=P))
 
         grouped = {}
@@ -129,7 +129,7 @@ def tile_mix_saveskip_relu_res_kernel(
                 banks[i, j] = psum.tile([P, CHUNK], F32, name="bank_%d_%d" % (i % 2, j))
             if s < 2:
                 weights = w8[:, s, tile_cols].bitcast(FP8X4)
-                weight_scales = w8_sc[:, s, tile_cols]
+                weight_scales = w8_sc[W8_PLANE:P, s, tile_cols]
             else:
                 weights = w4[:, 2 * j * P : 2 * (j + 1) * P].bitcast(FP4X4)
                 weight_scales = w4_sc[:, 0, tile_cols]
@@ -160,9 +160,9 @@ def tile_mix_saveskip_relu_res_kernel(
             nc.tensor.matmul_mx(
                 out=y[:],
                 lhsT=v8[:, j * P : (j + 1) * P].bitcast(FP8X4),
-                lhsT_scale=v8_sc[:, 0, j * P : (j + 1) * P],
+                lhsT_scale=v8_sc[V8_PLANE:P, 0, j * P : (j + 1) * P],
                 rhs=h_codes[:, cols(i)].bitcast(FP8X4),
-                rhs_scale=h_sc[:, cols(i)],
+                rhs_scale=h_sc[H_PLANE:P, cols(i)],
                 start=True,
                 stop=True,
             )
@@ -177,7 +177,7 @@ def tile_mix_saveskip_relu_res_kernel(
             quantize((i, s), codes[i, s][:], scales[i, s][:])
 
         def quantize_h(i):
-            quantize((i, "h"), h_codes[:, cols(i)], h_sc[:, cols(i)])
+            quantize((i, "h"), h_codes[:, cols(i)], h_sc[H_PLANE:P, cols(i)])
 
         nc.vector.tensor_copy(
             out=w8[:].bitcast(I32).rearrange("p a (j g i) -> p a g j i", j=PACK, i=4),
@@ -241,7 +241,7 @@ def tile_mix_saveskip_relu_res_kernel(
         nc.sync.dma_start(out=h_rows[:, :, CHUNK:T], in_=h_rest[:])
         nc.sync.dma_start(out=out_2[0].rearrange("p t i -> p (t i)").bitcast(I32), in_=h_codes[:].bitcast(I32))
         for j in range(PACK):
-            nc.sync.dma_start(
-                out=out_3[0].bitcast(I32)[4 * j : 4 * j + 4, :], in_=h_sc[32 * j : 32 * j + 4, :].bitcast(I32)
+            nc.gpsimd.dma_start(
+                out=out_3[0].bitcast(I32)[j:16:4, :], in_=h_sc[H_PLANE + j : P : 32, :].bitcast(I32)
             )
             nc.sync.dma_start(out=out_0[j * P : (j + 1) * P, :], in_=acc[:, j, :])

from contextlib import ExitStack

import concourse.mybir as mybir

K, L, R, N, T = 512, 1024, 512, 512, 1536
FLOPS = 2 * T * (K * R + L * R + R * N)

F32 = mybir.dt.float32
BF16 = mybir.dt.bfloat16
I32 = mybir.dt.int32
U32 = mybir.dt.uint32
U8 = mybir.dt.uint8
FP8X4 = mybir.dt.float8_e4m3fn_x4
FP4X4 = mybir.dt.float4_e2m1fn_x4

P = 128
PACK = 4
K_PASS = P * PACK
CHUNK = 512
CHUNKS = T // CHUNK
W8_PLANE = 12
V8_PLANE = 8
H_PLANE = 4
STREAMS = 3


def tile_mix_saveskip_relu_res_kernel(
    tc, x, c, w4_words, w4_scales, w8_words, w8_scales, v8_words, v8_scales, res, out_0, out_1, out_2, out_3
):
    nc = tc.nc
    with ExitStack() as ctx:
        keep = ctx.enter_context(tc.tile_pool(name="keep", bufs=1))
        stage = ctx.enter_context(tc.tile_pool(name="stage", bufs=6))
        psum = ctx.enter_context(tc.psum_pool(name="psum", bufs=1))
        ctx.enter_context(tc.manual_schedule())

        def cols(i):
            return slice(i * CHUNK, (i + 1) * CHUNK)

        w8_raw = keep.tile([P, 2, R], U32, name="w8_raw", align_bytes=64)
        w8_raw_sc = keep.tile([P, 2, R], U8, name="w8_raw_sc", align_bytes=64)
        w4_raw = keep.tile([P, 2 * R], U8, name="w4_raw", align_bytes=64)
        w4_raw_sc = keep.tile([P, 1, R], U8, name="w4_raw_sc", align_bytes=64)
        w8 = keep.tile([P, 2, R], U32, name="w8", align_bytes=64)
        w8_sc = keep.tile([P, 2, R], U8, name="w8_sc", align_bytes=64)
        w4 = keep.tile([P, 2 * R], U8, name="w4", align_bytes=64)
        w4_sc = keep.tile([P, 1, R], U8, name="w4_sc", align_bytes=64)
        v8 = keep.tile([P, N], U32, name="v8", align_bytes=64)
        v8_sc = keep.tile([P, 1, N], U8, name="v8_sc", align_bytes=64)

        raw = [keep.tile([P, PACK, T], F32, name="raw_%d" % s, align_bytes=64) for s in range(STREAMS - 1)]
        x_first = keep.tile([P, PACK, CHUNK], F32, name="x_first", align_bytes=64)
        x_rest = keep.tile([P, PACK, T - CHUNK], F32, name="x_rest", align_bytes=64)
        codes = {}
        scales = {}
        for i in range(CHUNKS):
            for s in range(STREAMS):
                codes[i, s] = keep.tile([P, CHUNK], U32, name="codes_%d_%d" % (i, s), align_bytes=64)
                scales[i, s] = keep.tile([P, CHUNK], U8, name="scales_%d_%d" % (i, s), align_bytes=64)
        acc = keep.tile([P, PACK, T], F32, name="acc", align_bytes=64)
        h_first = keep.tile([P, PACK, CHUNK], F32, name="h_first", align_bytes=64)
        h_rest = keep.tile([P, PACK, T - CHUNK], F32, name="h_rest", align_bytes=64)
        h_codes = keep.tile([P, T], U32, name="h_codes", align_bytes=64)
        h_sc = keep.tile([P, T], U8, name="h_sc", align_bytes=64)

        def h_chunk(i):
            return h_first[:] if i == 0 else h_rest[:, :, cols(i - 1)]

        def raw_chunk(i, s):
            if s < 2:
                return raw[s][:, :, cols(i)]
            return x_first[:] if i == 0 else x_rest[:, :, cols(i - 1)]

        stream_rows = [c[0:K_PASS, :], c[K_PASS:L, :]]
        x_rows = x.rearrange("(p j) t -> p j t", j=PACK)

        def load_stream(s):
            nc.sync.dma_start(out=raw[s][:], in_=stream_rows[s].rearrange("(p j) t -> p j t", j=PACK))

        def load_scale_rows(plane, first, dram):
            for r in range(4):
                nc.gpsimd.dma_start(
                    out=plane[first + r : P : 32, :, :].bitcast(I32),
                    in_=dram.bitcast(I32)[:, r:16:4, :].rearrange("a q n -> q a n"),
                )

        for plane in (w8_raw_sc, w4_raw_sc, v8_sc):
            nc.vector.memset(plane[:].bitcast(I32), 0)
        load_scale_rows(w8_raw_sc, W8_PLANE, w8_scales)
        load_scale_rows(w4_raw_sc, 0, w4_scales)
        load_scale_rows(v8_sc, V8_PLANE, v8_scales)

        nc.sync.dma_start(out=w8_raw[:].bitcast(I32), in_=w8_words.rearrange("a p r i -> p a (r i)").bitcast(I32))
        load_stream(0)
        nc.sync.dma_start(out=w4_raw[:].bitcast(I32), in_=w4_words[0].bitcast(I32))
        load_stream(1)
        nc.sync.dma_start(out=x_first[:], in_=x_rows[:, :, 0:CHUNK])
        nc.sync.dma_start(out=x_rest[:], in_=x_rows[:, :, CHUNK:T])
        nc.sync.dma_start(out=v8[:].bitcast(I32), in_=v8_words[0].rearrange("p n i -> p (n i)").bitcast(I32))
        nc.sync.dma_start(out=acc[:], in_=res.rearrange("(j p) t -> p j t", p=P))

        grouped = {}

        def interleave(key, src, on_scalar):
            grouped[key] = stage.tile([P, CHUNK, PACK], BF16, name="grouped", align_bytes=64)
            dst_view = grouped[key][:].rearrange("p (g i) j -> p g j i", i=4)
            src_view = src.rearrange("p j (g i) -> p g j i", i=4)
            if on_scalar:
                nc.scalar.copy(out=dst_view, in_=src_view)
            else:
                nc.vector.tensor_copy(out=dst_view, in_=src_view)

        def quantize(key, words, plane):
            nc.vector.quantize_mx(
                out=words.bitcast(FP8X4), scales=plane, in_=grouped[key][:].rearrange("p t j -> p (t j)")
            )

        def deal_scales(dst, src):
            nc.vector.tensor_copy(
                out=dst[:].rearrange("p a (j g i) -> p a g j i", j=PACK, i=16),
                in_=src[:].rearrange("p a (g i j) -> p a g j i", j=PACK, i=16),
            )

        banks = {}

        def first_layer(i, s, j):
            tile_cols = slice(j * P, (j + 1) * P)
            if s == 0:
                banks[i, j] = psum.tile([P, CHUNK], F32, name="bank_%d_%d" % (i % 2, j))
            if s < 2:
                weights = w8[:, s, tile_cols].bitcast(FP8X4)
                weight_scales = w8_sc[W8_PLANE:P, s, tile_cols]
            else:
                weights = w4[:, 2 * j * P : 2 * (j + 1) * P].bitcast(FP4X4)
                weight_scales = w4_sc[:, 0, tile_cols]
            nc.tensor.matmul_mx(
                out=banks[i, j][:],
                lhsT=weights,
                lhsT_scale=weight_scales,
                rhs=codes[i, s][:].bitcast(FP8X4),
                rhs_scale=scales[i, s][:],
                start=(s == 0),
                stop=(s == STREAMS - 1),
            )

        def first_layer_pass(i, s):
            for j in range(PACK):
                first_layer(i, s, j)

        def relu(i, j, on_scalar):
            if on_scalar:
                nc.scalar.activation(
                    out=h_chunk(i)[:, j, :], in_=banks[i, j][:], func=mybir.ActivationFunctionType.Relu
                )
            else:
                nc.vector.tensor_scalar_max(out=h_chunk(i)[:, j, :], in0=banks[i, j][:], scalar1=0.0)

        def second_layer(j, i, bank):
            y = psum.tile([P, CHUNK], F32, name="bank_1_%d" % bank)
            nc.tensor.matmul_mx(
                out=y[:],
                lhsT=v8[:, j * P : (j + 1) * P].bitcast(FP8X4),
                lhsT_scale=v8_sc[V8_PLANE:P, 0, j * P : (j + 1) * P],
                rhs=h_codes[:, cols(i)].bitcast(FP8X4),
                rhs_scale=h_sc[H_PLANE:P, cols(i)],
                start=True,
                stop=True,
            )
            nc.vector.tensor_tensor(
                out=acc[:, j, cols(i)], in0=y[:], in1=acc[:, j, cols(i)], op=mybir.AluOpType.add
            )

        def interleave_stream(i, s, on_scalar):
            interleave((i, s), raw_chunk(i, s), on_scalar)

        def quantize_stream(i, s):
            quantize((i, s), codes[i, s][:], scales[i, s][:])

        def quantize_h(i):
            quantize((i, "h"), h_codes[:, cols(i)], h_sc[H_PLANE:P, cols(i)])

        nc.vector.tensor_copy(
            out=w8[:].bitcast(I32).rearrange("p a (j g i) -> p a g j i", j=PACK, i=4),
            in_=w8_raw[:].bitcast(I32).rearrange("p a (g i j) -> p a g j i", j=PACK, i=4),
        )
        interleave_stream(1, 0, True)
        interleave_stream(2, 0, True)
        interleave_stream(0, 0, False)
        deal_scales(w8_sc, w8_raw_sc)
        quantize_stream(0, 0)
        nc.vector.tensor_copy(
            out=w4[:].rearrange("p (j g i b) -> p g j i b", j=PACK, i=8, b=2),
            in_=w4_raw[:].rearrange("p (g i j b) -> p g j i b", j=PACK, i=8, b=2),
        )
        quantize_stream(1, 0)
        quantize_stream(2, 0)
        first_layer_pass(0, 0)
        first_layer_pass(1, 0)

        interleave_stream(1, 1, True)
        interleave_stream(2, 1, True)
        interleave_stream(0, 1, False)
        deal_scales(w4_sc, w4_raw_sc)
        quantize_stream(0, 1)
        first_layer_pass(0, 1)
        interleave_stream(0, 2, False)
        quantize_stream(1, 1)
        first_layer_pass(1, 1)
        quantize_stream(0, 2)
        quantize_stream(2, 1)
        first_layer_pass(0, 2)
        for j in range(PACK):
            relu(0, j, True)
        first_layer_pass(2, 0)
        first_layer_pass(2, 1)
        interleave((0, "h"), h_chunk(0), True)
        for i in (1, 2):
            interleave_stream(i, 2, False)
            quantize_stream(i, 2)
            first_layer_pass(i, 2)
        quantize_h(0)
        for j in range(PACK):
            relu(1, j, True)
        for j in range(PACK):
            relu(2, j, j % 2 == 1)
        interleave((1, "h"), h_chunk(1), False)
        interleave((2, "h"), h_chunk(2), True)
        second_layer(0, 0, 0)
        quantize_h(1)
        second_layer(1, 0, 1)
        second_layer(0, 1, 2)
        quantize_h(2)
        second_layer(1, 1, 3)
        second_layer(0, 2, 0)
        second_layer(1, 2, 1)
        for n in range(2 * CHUNKS):
            second_layer(2 + n // CHUNKS, n % CHUNKS, (2 + n) % PACK)

        h_rows = out_1.rearrange("(p j) t -> p j t", j=PACK)
        nc.sync.dma_start(out=h_rows[:, :, 0:CHUNK], in_=h_first[:])
        nc.sync.dma_start(out=h_rows[:, :, CHUNK:T], in_=h_rest[:])
        nc.sync.dma_start(out=out_2[0].rearrange("p t i -> p (t i)").bitcast(I32), in_=h_codes[:].bitcast(I32))
        for j in range(PACK):
            nc.gpsimd.dma_start(
                out=out_3[0].bitcast(I32)[j:16:4, :], in_=h_sc[H_PLANE + j : P : 32, :].bitcast(I32)
            )
            nc.sync.dma_start(out=out_0[j * P : (j + 1) * P, :], in_=acc[:, j, :])
